import numpy as np
import ml_dtypes


def mxq(x, axis, fmt="e4m3"):
    dtype, down = {"e4m3": (ml_dtypes.float8_e4m3fn, 7), "e5m2": (ml_dtypes.float8_e5m2, 14)}[fmt]
    v = np.moveaxis(np.asarray(x, np.float32).astype(ml_dtypes.bfloat16).astype(np.float64), axis, -1)
    blocks = v.reshape(v.shape[:-1] + (-1, 32))
    amax = np.abs(blocks).max(-1, keepdims=True)
    byte = np.maximum(np.where(amax > 0, np.frexp(amax)[1] - 1 + 127, 0) - down, 1)
    scale = np.exp2(byte - 127.0)
    codes = (blocks / scale).astype(np.float32).astype(dtype).astype(np.float64)
    return np.moveaxis((codes * scale).reshape(v.shape), -1, axis)


WIDE = False


def mx_kscale(k):
    if not WIDE:
        return np.ones(k)
    levels = np.array([10, -10, 5, -5, 0])
    if k % 512:
        return np.exp2(np.random.permutation(np.resize(levels, k // 32))).repeat(32)
    a = np.empty((k // 512, 16))
    for p in range(k // 512):
        a[p, :8] = np.random.permutation(np.resize(levels, 8))
        for g in range(8):
            far = levels[np.abs(levels - a[p, g]) >= 10]
            a[p, g + 8] = far[np.random.randint(len(far))]
    return np.exp2(a.ravel()).repeat(32)


def f64(x):
    return np.asarray(x).astype(np.float64)


def striped(idx):
    return np.tile(idx.reshape(-1, 16).T, (8, 1)).astype(np.uint16)


def unstriped(offs):
    return offs[:16].T.reshape(-1).astype(np.int64)


def striped8(idx):
    return np.concatenate([x.reshape(-1, 16).T for x in idx]).astype(np.uint16)


def runs(offs, k):
    lists = np.stack([offs[16 * r : 16 * r + 16].T.reshape(-1) for r in range(8)]).astype(np.int64)
    return lists[np.arange(k) % 512 // 64]


def pack_weight(w):
    k, n = w.shape
    w = f64(np.asarray(w, np.float32).astype(ml_dtypes.bfloat16)).reshape(k // 32, 32, n)
    amax = np.abs(w).max(1)
    byte = np.clip(np.where(amax > 0, np.frexp(amax)[1] - 1 + 127 - 7, 1), 1, 254)
    scaled = (w * np.exp2(127.0 - byte)[:, None, :]).reshape(k, n).astype(np.float32)
    words = np.ascontiguousarray(scaled.reshape(k // 512, 128, 4, n).transpose(0, 1, 3, 2)).astype(ml_dtypes.float8_e4m3fn).view(np.uint8)
    return words, np.ascontiguousarray(byte.astype(np.uint8).reshape(k // 512, 16, n))


def unpack_weight(words, scales):
    g, p, n, _ = words.shape
    vals = np.ascontiguousarray(words).view(ml_dtypes.float8_e4m3fn).astype(np.float64) * np.repeat(np.exp2(scales.astype(np.float64) - 127.0), 8, axis=1)[..., None]
    return vals.transpose(0, 1, 3, 2).reshape(g * 512, n)


K, T, S, N, H, U = 512, 2048, 512, 512, 512, 1024


def setup_inputs():
    n = np.random.standard_normal
    s = mx_kscale(K)[:, None]
    u = mx_kscale(H)
    packed_xT = pack_weight(n((K, T)) * s)
    return {
        "x_words": packed_xT[0],
        "x_scales": packed_xT[1],
        "w1": (n((K, H)) / np.sqrt(K) / s).astype(np.float32),
        "gn": (np.random.uniform(0.5, 1.5, (H, 1)) * u[:, None]).astype(np.float32),
        "w2": (n((H, N)) / np.sqrt(H) / u[:, None]).astype(np.float32),
        "pg": n((N, U)).astype(np.float32),
        "offs": striped(np.random.permutation(T)[:S]),
        "n1": striped8(np.stack([np.random.permutation(S) for _ in range(8)])),
        "slot": striped8(np.stack([np.random.permutation(U)[:S] for _ in range(8)])),
    }


def reference(x_words, x_scales, w1, gn, w2, pg, offs, n1, slot):
    xq = unpack_weight(x_words, x_scales)[:, unstriped(offs)]
    y = mxq(f64(w1), 0, "e4m3").T @ xq
    pw = (y) ** 2
    z = f64(gn) * (y * (np.exp(-0.5 * (pw[np.arange(H)[:, None], runs(n1, H)]))))
    h = mxq(f64(w2), 0, "e4m3").T @ mxq(z, 0, "e4m3")
    nw = f64(pg)[np.arange(N)[:, None], runs(slot, N)] + 0.5 * (np.tanh(h - (f64(pg)[np.arange(N)[:, None], runs(slot, N)])))
    out = f64(pg).copy()
    out[np.arange(N)[:, None], runs(slot, N)] = nw
    return out

@@ -1,0 +1,212 @@
+from contextlib import ExitStack
+
+import concourse.mybir as mybir
+from concourse.masks import make_identity
+
+K, T, S, N, H, U = 512, 2048, 512, 512, 512, 1024
+FLOPS = 2 * K * H * S + 2 * H * N * S
+
+F32 = mybir.dt.float32
+BF16 = mybir.dt.bfloat16
+I32 = mybir.dt.int32
+U32 = mybir.dt.uint32
+U16 = mybir.dt.uint16
+U8 = mybir.dt.uint8
+FP8X4 = mybir.dt.float8_e4m3fn_x4
+ALU = mybir.AluOpType
+ACT = mybir.ActivationFunctionType
+
+P = 128
+PACK = 4
+HALF = S // 2
+LIST_COLS = HALF // 16
+BANK = 512
+
+
+def tile_picked_masktrack_none_p_kernel(tc, x_words, x_scales, w1, gn, w2, pg, offs, n1, slot, out):
+    nc = tc.nc
+    with ExitStack() as ctx:
+        keep = ctx.enter_context(tc.tile_pool(name="keep", bufs=1))
+        psum = ctx.enter_context(tc.psum_pool(name="psum", bufs=2))
+
+        def sb(name, shape, dtype, tag=""):
+            return keep.tile(shape, dtype, name=name, tag=tag, align_bytes=64)
+
+        def bank():
+            return psum.tile([P, BANK], F32, name="bank", bufs=4)
+
+        offs_t = sb("offs_t", [P, S // 16], U16)
+        n1_t = sb("n1_t", [P, S // 16], U16)
+        slot_t = sb("slot_t", [P, S // 16], U16)
+        xw = sb("xw", [P, T], U32)
+        xs = sb("xs", [P, T], U8)
+        w1_raw = sb("w1_raw", [P, PACK, H], F32)
+        w2_raw = sb("w2_raw", [P, PACK, N], F32)
+        gn_t = sb("gn_t", [P, PACK], F32)
+        page = [sb("page%d" % t, [P, U], F32) for t in range(PACK)]
+        ident = sb("ident", [P, P], F32)
+        warm = sb("warm", [P, 1], F32)
+
+        nc.gpsimd.memset(xs[:].bitcast(I32), 0)
+        make_identity(nc, ident[:])
+
+        pg_rows = pg.rearrange("(p t) u -> p t u", t=PACK)
+        out_rows = out.rearrange("(p t) u -> p t u", t=PACK)
+        nc.sync.dma_start(offs_t[:], offs)
+        nc.sync.dma_start(w1_raw[:], w1.rearrange("(p j) c -> p j c", j=PACK))
+        for q in range(4):
+            nc.scalar.dma_start(xs[32 * q : 32 * q + 4, :].bitcast(I32), x_scales[0, 4 * q : 4 * q + 4, :].bitcast(I32))
+        nc.scalar.activation(warm[:], ident[:, 0:1], ACT.Exp)
+        nc.sync.dma_start(xw[:].bitcast(I32), x_words[0].rearrange("p n r -> p (n r)").bitcast(I32))
+        nc.sync.dma_start(slot_t[:], slot)
+        nc.sync.dma_start(n1_t[:], n1)
+        nc.sync.dma_start(gn_t[:], gn.rearrange("(p t) o -> p (t o)", t=PACK))
+        for t in range(PACK):
+            nc.sync.dma_start(page[t][:], pg_rows[:, t, :])
+        nc.sync.dma_start(w2_raw[:], w2.rearrange("(p j) c -> p j c", j=PACK))
+
+        def deal(raw, pair, name, engine, tag=""):
+            grouped = sb("%s_bf%d" % (name, pair), [P, 2 * P * PACK], BF16, tag)
+            dst = grouped[:].rearrange("p (t m j) -> p m j t", t=2, j=PACK)
+            src = raw[:].rearrange("p j (m t) -> p m j t", t=PACK)[:, :, :, 2 * pair : 2 * pair + 2]
+            if engine == "scalar":
+                nc.scalar.copy(dst, src)
+            else:
+                nc.vector.tensor_copy(dst, src)
+            return grouped
+
+        def quantize(grouped, name):
+            width = grouped.shape[1] // PACK
+            codes = sb(name + "_codes", [P, width], U32)
+            scales = sb(name + "_scales", [P, width], U8)
+            nc.vector.quantize_mx(out=codes[:].bitcast(FP8X4), scales=scales[:], in_=grouped[:])
+            return codes, scales
+
+        def product(dst, weights, i, codes, scales):
+            cols = slice(i * P, (i + 1) * P)
+            nc.tensor.matmul_mx(out=dst, lhsT=weights[0][:, cols].bitcast(FP8X4), lhsT_scale=weights[1][:, cols],
+                                rhs=codes.bitcast(FP8X4), rhs_scale=scales, start=True, stop=True)
+
+        def entries(lst, h):
+            return lst[:, h * LIST_COLS : (h + 1) * LIST_COLS]
+
+        gs = sb("gs", [P, S], U8)
+        nc.vector.tensor_copy(gs[:], xs[:].indirect(offs_t[:]))
+        w1_bf = [deal(w1_raw, 0, "w1", "vector"), deal(w1_raw, 1, "w1", "scalar")]
+        w1_q = [quantize(w1_bf[pair], "w1_%d" % pair) for pair in range(2)]
+        pw = [sb("pw%d" % t, [P, S], F32) for t in range(PACK)]
+        y = {}
+        for h in range(2):
+            gw = sb("gw%d" % h, [P, HALF], U32)
+            nc.vector.tensor_copy(gw[:], xw[:].indirect(entries(offs_t, h)))
+            for pair in range(2):
+                acc = bank()
+                for i in range(2):
+                    y[h, 2 * pair + i] = acc[:, i * HALF : (i + 1) * HALF]
+                    product(y[h, 2 * pair + i], w1_q[pair], i, gw[:], gs[:, h * HALF : (h + 1) * HALF])
+            for t in range(PACK):
+                nc.scalar.activation(pw[t][:, h * HALF : (h + 1) * HALF], y[h, t], ACT.Square)
+
+        old = [sb("old%d" % t, [P, S], F32) for t in range(PACK)]
+        for t in range(PACK):
+            nc.vector.tensor_copy(old[t][:], page[t][:].indirect(slot_t[:]))
+
+        def gate(h):
+            e = [sb("e%d_%d" % (h, t), [P, HALF], F32) for t in range(PACK)]
+            for t in range(PACK):
+                nc.scalar.activation(e[t][:], pw[t][:].indirect(entries(n1_t, h)), ACT.Exp, scale=-0.5)
+            return e
+
+        def z_planes(h, e, planes, tiles):
+            for t in tiles:
+                nc.vector.scalar_tensor_tensor(planes[:, t * HALF : (t + 1) * HALF], y[h, t], gn_t[:, t : t + 1], e[t][:], ALU.mult, ALU.mult)
+
+        def z_weave(h, planes, engine):
+            grouped = sb("z_bf%d" % h, [P, PACK * HALF], BF16)
+            dst = grouped[:].rearrange("p (c i t) -> p c t i", i=4, t=PACK)
+            src = planes[:].rearrange("p (t c i) -> p c t i", i=4, t=PACK)
+            if engine == "scalar":
+                nc.scalar.copy(dst, src)
+            else:
+                nc.vector.tensor_copy(dst, src)
+            return grouped
+
+        hh = {}
+
+        def second(h, pair, zq):
+            acc = bank()
+            for i in range(2):
+                hh[h, 2 * pair + i] = acc[:, i * HALF : (i + 1) * HALF]
+                product(hh[h, 2 * pair + i], w2_q[pair], i, zq[0][:], zq[1][:])
+
+        def step_vector(h, t):
+            return finish(h, t, subtract(h, t))
+
+        def subtract(h, t):
+            diff = sb("diff%d_%d" % (h, t), [P, HALF], F32)
+            nc.vector.tensor_tensor(diff[:], hh[h, t], old[t][:, h * HALF : (h + 1) * HALF], ALU.subtract)
+            return diff
+
+        def finish(h, t, diff):
+            th = sb("th%d_%d" % (h, t), [P, HALF], F32)
+            nc.scalar.activation(th[:], diff[:], ACT.Tanh)
+            step = sb("step%d_%d" % (h, t), [P, HALF], F32)
+            nc.scalar.activation(step[:], th[:], ACT.Copy, scale=0.5)
+            return step
+
+        def step_tensor(h, t):
+            neg = sb("neg%d_%d" % (h, t), [P, HALF], F32)
+            nc.scalar.activation(neg[:], hh[h, t], ACT.Copy, scale=-1.0)
+            turned = psum.tile([P, HALF], F32, name="turned")
+            for b in range(2):
+                cols = slice(b * P, (b + 1) * P)
+                first = h * HALF + b * P
+                nc.tensor.matmul(turned[:, cols], old[t][:, first : first + P], ident[:], start=True, stop=False, is_transpose=True)
+                nc.tensor.matmul(turned[:, cols], neg[:, cols], ident[:], start=False, stop=True, is_transpose=True)
+            th = sb("th%d_%d" % (h, t), [P, HALF], F32)
+            nc.scalar.activation(th[:], turned[:], ACT.Tanh, scale=-1.0)
+            back = psum.tile([P, HALF], F32, name="back")
+            for b in range(2):
+                cols = slice(b * P, (b + 1) * P)
+                nc.tensor.transpose(back[:, cols], th[:, cols], ident[:])
+            step = sb("step%d_%d" % (h, t), [P, HALF], F32)
+            nc.scalar.activation(step[:], back[:], ACT.Copy, scale=0.5)
+            return step
+
+        def put(h, t, step):
+            nc.vector.tensor_tensor(page[t][:].indirect(entries(slot_t, h)), old[t][:, h * HALF : (h + 1) * HALF], step[:], ALU.add)
+            if h == 1:
+                nc.sync.dma_start(out_rows[:, t, :], page[t][:])
+
+        ON_VECTOR = (0,1,)
+
+        def step_of(h, t):
+            return step_vector(h, t) if 4 * h + t in ON_VECTOR else step_tensor(h, t)
+
+        e0 = gate(0)
+        e1 = gate(1)
+        planes0 = sb("zp0", [P, PACK * HALF], BF16)
+        z_planes(0, e0, planes0, range(PACK))
+        woven0 = z_weave(0, planes0, "vector")
+        w2_bf = [deal(w2_raw, 0, "w2", "vector", "held"), deal(w2_raw, 1, "w2", "scalar")]
+        z0 = quantize(woven0, "z0")
+        w2_q = {0: quantize(w2_bf[0], "w2_0")}
+        second(0, 0, z0)
+        steps = {}
+        steps[0, 0] = step_of(0, 0)
+        planes1 = sb("zp1", [P, PACK * HALF], BF16, "held")
+        z_planes(1, e1, planes1, (0, 1))
+        w2_q[1] = quantize(w2_bf[1], "w2_1")
+        second(0, 1, z0)
+        z_planes(1, e1, planes1, (2, 3))
+        woven1 = z_weave(1, planes1, "scalar")
+        for t in range(1, PACK):
+            steps[0, t] = step_of(0, t)
+        z1 = quantize(woven1, "z1")
+        second(1, 0, z1)
+        second(1, 1, z1)
+        for t in range(PACK):
+            put(0, t, steps[0, t])
+            steps[1, t] = step_of(1, t)
+        for t in range(PACK):
+            put(1, t, steps[1, t])

@@ -1,7 +1,6 @@
 from contextlib import ExitStack
 
 import concourse.mybir as mybir
-from concourse.masks import make_identity
 
 K, T, S, N, H, U = 512, 2048, 512, 512, 512, 1024
 FLOPS = 2 * K * H * S + 2 * H * N * S
@@ -47,15 +46,15 @@ def tile_picked_masktrack_none_p_kernel(tc, x_words, x_scales, w1, gn, w2, pg, o
         ident = sb("ident", [P, P], F32)
         warm = sb("warm", [P, 1], F32)
 
-        nc.gpsimd.memset(xs[:].bitcast(I32), 0)
-        make_identity(nc, ident[:])
+        nc.vector.memset(xs[:].bitcast(I32), 0)
+        nc.gpsimd.memset(ident[:, 0:1], 0.0)
 
         pg_rows = pg.rearrange("(p t) u -> p t u", t=PACK)
         out_rows = out.rearrange("(p t) u -> p t u", t=PACK)
         nc.sync.dma_start(offs_t[:], offs)
         nc.sync.dma_start(w1_raw[:], w1.rearrange("(p j) c -> p j c", j=PACK))
         for q in range(4):
-            nc.scalar.dma_start(xs[32 * q : 32 * q + 4, :].bitcast(I32), x_scales[0, 4 * q : 4 * q + 4, :].bitcast(I32))
+            nc.sync.dma_start(xs[32 * q : 32 * q + 4, :].bitcast(I32), x_scales[0, 4 * q : 4 * q + 4, :].bitcast(I32))
         nc.scalar.activation(warm[:], ident[:, 0:1], ACT.Exp)
         nc.sync.dma_start(xw[:].bitcast(I32), x_words[0].rearrange("p n r -> p (n r)").bitcast(I32))
         nc.sync.dma_start(slot_t[:], slot)
@@ -122,7 +121,7 @@ def tile_picked_masktrack_none_p_kernel(tc, x_words, x_scales, w1, gn, w2, pg, o
                 nc.vector.scalar_tensor_tensor(planes[:, t * HALF : (t + 1) * HALF], y[h, t], gn_t[:, t : t + 1], e[t][:], ALU.mult, ALU.mult)
 
         def z_weave(h, planes, engine):
-            grouped = sb("z_bf%d" % h, [P, PACK * HALF], BF16)
+            grouped = sb("z_bf%d" % h, [P, PACK * HALF], BF16, "after_first" if h == 1 else "")
             dst = grouped[:].rearrange("p (c i t) -> p c t i", i=4, t=PACK)
             src = planes[:].rearrange("p (t c i) -> p c t i", i=4, t=PACK)
             if engine == "scalar":
@@ -148,7 +147,7 @@ def tile_picked_masktrack_none_p_kernel(tc, x_words, x_scales, w1, gn, w2, pg, o
             return diff
 
         def finish(h, t, diff):
-            th = sb("th%d_%d" % (h, t), [P, HALF], F32)
+            th = sb("th%d_%d" % (h, t), [P, HALF], F32, "after_first" if (h, t) == (0, 0) else "")
             nc.scalar.activation(th[:], diff[:], ACT.Tanh)
             step = sb("step%d_%d" % (h, t), [P, HALF], F32)
             nc.scalar.activation(step[:], th[:], ACT.Copy, scale=0.5)
@@ -178,7 +177,7 @@ def tile_picked_masktrack_none_p_kernel(tc, x_words, x_scales, w1, gn, w2, pg, o
             if h == 1:
                 nc.sync.dma_start(out_rows[:, t, :], page[t][:])
 
-        ON_VECTOR = (0,1,)
+        ON_VECTOR = (0,1,2,3,4,5,6,7,)
 
         def step_of(h, t):
             return step_vector(h, t) if 4 * h + t in ON_VECTOR else step_tensor(h, t)

@@ -1,6 +1,7 @@
 from contextlib import ExitStack
 
 import concourse.mybir as mybir
+from concourse.masks import make_identity
 
 K, T, S, N, H, U = 512, 2048, 512, 512, 512, 1024
 FLOPS = 2 * K * H * S + 2 * H * N * S
@@ -47,7 +48,7 @@ def tile_picked_masktrack_none_p_kernel(tc, x_words, x_scales, w1, gn, w2, pg, o
         warm = sb("warm", [P, 1], F32)
 
         nc.vector.memset(xs[:].bitcast(I32), 0)
-        nc.gpsimd.memset(ident[:, 0:1], 0.0)
+        make_identity(nc, ident[:])
 
         pg_rows = pg.rearrange("(p t) u -> p t u", t=PACK)
         out_rows = out.rearrange("(p t) u -> p t u", t=PACK)
@@ -59,9 +60,9 @@ def tile_picked_masktrack_none_p_kernel(tc, x_words, x_scales, w1, gn, w2, pg, o
         nc.sync.dma_start(xw[:].bitcast(I32), x_words[0].rearrange("p n r -> p (n r)").bitcast(I32))
         nc.sync.dma_start(slot_t[:], slot)
         nc.sync.dma_start(n1_t[:], n1)
-        nc.sync.dma_start(gn_t[:], gn.rearrange("(p t) o -> p (t o)", t=PACK))
         for t in range(PACK):
             nc.sync.dma_start(page[t][:], pg_rows[:, t, :])
+        nc.sync.dma_start(gn_t[:], gn.rearrange("(p t) o -> p (t o)", t=PACK))
         nc.sync.dma_start(w2_raw[:], w2.rearrange("(p j) c -> p j c", j=PACK))
 
         def deal(raw, pair, name, engine, tag=""):
@@ -70,6 +71,8 @@ def tile_picked_masktrack_none_p_kernel(tc, x_words, x_scales, w1, gn, w2, pg, o
             src = raw[:].rearrange("p j (m t) -> p m j t", t=PACK)[:, :, :, 2 * pair : 2 * pair + 2]
             if engine == "scalar":
                 nc.scalar.copy(dst, src)
+            elif engine == "gpsimd":
+                nc.gpsimd.tensor_scalar(dst, src, 1.0, 0.0, ALU.mult, ALU.add)
             else:
                 nc.vector.tensor_copy(dst, src)
             return grouped
@@ -136,6 +139,8 @@ def tile_picked_masktrack_none_p_kernel(tc, x_words, x_scales, w1, gn, w2, pg, o
             acc = bank()
             for i in range(2):
                 hh[h, 2 * pair + i] = acc[:, i * HALF : (i + 1) * HALF]
+                if (h, pair, i) == (0, 0, 0):
+                    hh[0, 0] = psum.tile([P, HALF], F32, name="back")[:]
                 product(hh[h, 2 * pair + i], w2_q[pair], i, zq[0][:], zq[1][:])
 
         def step_vector(h, t):
@@ -177,7 +182,7 @@ def tile_picked_masktrack_none_p_kernel(tc, x_words, x_scales, w1, gn, w2, pg, o
             if h == 1:
                 nc.sync.dma_start(out_rows[:, t, :], page[t][:])
 
-        ON_VECTOR = (0,1,2,3,4,5,6,7,)
+        ON_VECTOR = (0,1,)
 
         def step_of(h, t):
             return step_vector(h, t) if 4 * h + t in ON_VECTOR else step_tensor(h, t)

@@ -182,7 +182,7 @@ def tile_picked_masktrack_none_p_kernel(tc, x_words, x_scales, w1, gn, w2, pg, o
             if h == 1:
                 nc.sync.dma_start(out_rows[:, t, :], page[t][:])
 
-        ON_VECTOR = (0,1,)
+        ON_VECTOR = (0,1,2,4,)
 
         def step_of(h, t):
             return step_vector(h, t) if 4 * h + t in ON_VECTOR else step_tensor(h, t)
@@ -204,7 +204,7 @@ def tile_picked_masktrack_none_p_kernel(tc, x_words, x_scales, w1, gn, w2, pg, o
         second(0, 1, z0)
         z_planes(1, e1, planes1, (2, 3))
         woven1 = z_weave(1, planes1, "scalar")
-        for t in range(1, PACK):
+        for t in (1, 3, 2):
             steps[0, t] = step_of(0, t)
         z1 = quantize(woven1, "z1")
         second(1, 0, z1)

@@ -20,197 +20,205 @@ P = 128
 PACK = 4
 HALF = S // 2
 LIST_COLS = HALF // 16
-BANK = 512
+PAIR_BANKS = 4
+TURN_BANKS = 2
+
+SUBTRACT_ON_VECTOR = ((0, 0), (0, 1), (0, 2), (1, 0))
 
 
 def tile_picked_masktrack_none_p_kernel(tc, x_words, x_scales, w1, gn, w2, pg, offs, n1, slot, out):
     nc = tc.nc
     with ExitStack() as ctx:
         keep = ctx.enter_context(tc.tile_pool(name="keep", bufs=1))
-        psum = ctx.enter_context(tc.psum_pool(name="psum", bufs=2))
+        psum = ctx.enter_context(tc.psum_pool(name="psum", bufs=TURN_BANKS))
 
-        def sb(name, shape, dtype, tag=""):
+        def sbuf(name, shape, dtype, tag=""):
             return keep.tile(shape, dtype, name=name, tag=tag, align_bytes=64)
 
-        def bank():
-            return psum.tile([P, BANK], F32, name="bank", bufs=4)
+        def pair_bank():
+            return psum.tile([P, 2 * HALF], F32, name="pair_bank", bufs=PAIR_BANKS)
 
-        offs_t = sb("offs_t", [P, S // 16], U16)
-        n1_t = sb("n1_t", [P, S // 16], U16)
-        slot_t = sb("slot_t", [P, S // 16], U16)
-        xw = sb("xw", [P, T], U32)
-        xs = sb("xs", [P, T], U8)
-        w1_raw = sb("w1_raw", [P, PACK, H], F32)
-        w2_raw = sb("w2_raw", [P, PACK, N], F32)
-        gn_t = sb("gn_t", [P, PACK], F32)
-        page = [sb("page%d" % t, [P, U], F32) for t in range(PACK)]
-        ident = sb("ident", [P, P], F32)
-        warm = sb("warm", [P, 1], F32)
+        def half_cols(half):
+            return slice(half * HALF, (half + 1) * HALF)
 
-        nc.vector.memset(xs[:].bitcast(I32), 0)
-        make_identity(nc, ident[:])
+        def entries(list_tile, half):
+            return list_tile[:, half * LIST_COLS : (half + 1) * LIST_COLS]
+
+        offs_t = sbuf("offs_t", [P, S // 16], U16)
+        n1_t = sbuf("n1_t", [P, S // 16], U16)
+        slot_t = sbuf("slot_t", [P, S // 16], U16)
+        table_words = sbuf("table_words", [P, T], U32)
+        table_scales = sbuf("table_scales", [P, T], U8)
+        w1_raw = sbuf("w1_raw", [P, PACK, H], F32)
+        w2_raw = sbuf("w2_raw", [P, PACK, N], F32)
+        gn_t = sbuf("gn_t", [P, PACK], F32)
+        page = [sbuf("page%d" % t, [P, U], F32) for t in range(PACK)]
+        identity = sbuf("identity", [P, P], F32)
+
+        nc.vector.memset(table_scales[:].bitcast(I32), 0)
+        make_identity(nc, identity[:])
 
         pg_rows = pg.rearrange("(p t) u -> p t u", t=PACK)
         out_rows = out.rearrange("(p t) u -> p t u", t=PACK)
+        w2_rows = w2.rearrange("(p j) c -> p j c", j=PACK)
         nc.sync.dma_start(offs_t[:], offs)
         nc.sync.dma_start(w1_raw[:], w1.rearrange("(p j) c -> p j c", j=PACK))
         for q in range(4):
-            nc.sync.dma_start(xs[32 * q : 32 * q + 4, :].bitcast(I32), x_scales[0, 4 * q : 4 * q + 4, :].bitcast(I32))
-        nc.scalar.activation(warm[:], ident[:, 0:1], ACT.Exp)
-        nc.sync.dma_start(xw[:].bitcast(I32), x_words[0].rearrange("p n r -> p (n r)").bitcast(I32))
+            nc.sync.dma_start(table_scales[32 * q : 32 * q + 4, :].bitcast(I32), x_scales[0, 4 * q : 4 * q + 4, :].bitcast(I32))
+        nc.sync.dma_start(table_words[:].bitcast(I32), x_words[0].rearrange("p n r -> p (n r)").bitcast(I32))
         nc.sync.dma_start(slot_t[:], slot)
         nc.sync.dma_start(n1_t[:], n1)
         for t in range(PACK):
             nc.sync.dma_start(page[t][:], pg_rows[:, t, :])
+        nc.sync.dma_start(w2_raw[:, 0:2, :], w2_rows[:, 0:2, :])
         nc.sync.dma_start(gn_t[:], gn.rearrange("(p t) o -> p (t o)", t=PACK))
-        nc.sync.dma_start(w2_raw[:], w2.rearrange("(p j) c -> p j c", j=PACK))
+        nc.sync.dma_start(w2_raw[:, 2:4, :], w2_rows[:, 2:4, :])
 
-        def deal(raw, pair, name, engine, tag=""):
-            grouped = sb("%s_bf%d" % (name, pair), [P, 2 * P * PACK], BF16, tag)
+        def deal_views(raw, pair, name, tag=""):
+            grouped = sbuf("%s_bf%d" % (name, pair), [P, 2 * P * PACK], BF16, tag)
             dst = grouped[:].rearrange("p (t m j) -> p m j t", t=2, j=PACK)
             src = raw[:].rearrange("p j (m t) -> p m j t", t=PACK)[:, :, :, 2 * pair : 2 * pair + 2]
-            if engine == "scalar":
-                nc.scalar.copy(dst, src)
-            elif engine == "gpsimd":
-                nc.gpsimd.tensor_scalar(dst, src, 1.0, 0.0, ALU.mult, ALU.add)
-            else:
-                nc.vector.tensor_copy(dst, src)
-            return grouped
+            return grouped, dst, src
+
+        def deal(raw, name, first_tag=""):
+            first, dst, src = deal_views(raw, 0, name, first_tag)
+            nc.vector.tensor_copy(dst, src)
+            second, dst, src = deal_views(raw, 1, name)
+            nc.scalar.activation(dst, src, ACT.Copy)
+            return first, second
 
         def quantize(grouped, name):
             width = grouped.shape[1] // PACK
-            codes = sb(name + "_codes", [P, width], U32)
-            scales = sb(name + "_scales", [P, width], U8)
-            nc.vector.quantize_mx(out=codes[:].bitcast(FP8X4), scales=scales[:], in_=grouped[:])
-            return codes, scales
+            words = sbuf(name + "_words", [P, width], U32)
+            scales = sbuf(name + "_scales", [P, width], U8)
+            nc.vector.quantize_mx(out=words[:].bitcast(FP8X4), scales=scales[:], in_=grouped[:])
+            return words, scales
 
-        def product(dst, weights, i, codes, scales):
+        def product(dst, weights, i, words, scales):
             cols = slice(i * P, (i + 1) * P)
-            nc.tensor.matmul_mx(out=dst, lhsT=weights[0][:, cols].bitcast(FP8X4), lhsT_scale=weights[1][:, cols],
-                                rhs=codes.bitcast(FP8X4), rhs_scale=scales, start=True, stop=True)
+            nc.tensor.matmul_mx(
+                out=dst,
+                lhsT=weights[0][:, cols].bitcast(FP8X4),
+                lhsT_scale=weights[1][:, cols],
+                rhs=words.bitcast(FP8X4),
+                rhs_scale=scales,
+                start=True,
+                stop=True,
+            )
 
-        def entries(lst, h):
-            return lst[:, h * LIST_COLS : (h + 1) * LIST_COLS]
-
-        gs = sb("gs", [P, S], U8)
-        nc.vector.tensor_copy(gs[:], xs[:].indirect(offs_t[:]))
-        w1_bf = [deal(w1_raw, 0, "w1", "vector"), deal(w1_raw, 1, "w1", "scalar")]
+        picked_scales = sbuf("picked_scales", [P, S], U8)
+        nc.vector.tensor_copy(picked_scales[:], table_scales[:].indirect(offs_t[:]))
+        w1_bf = deal(w1_raw, "w1")
         w1_q = [quantize(w1_bf[pair], "w1_%d" % pair) for pair in range(2)]
-        pw = [sb("pw%d" % t, [P, S], F32) for t in range(PACK)]
+        pw = [sbuf("pw%d" % t, [P, S], F32) for t in range(PACK)]
         y = {}
-        for h in range(2):
-            gw = sb("gw%d" % h, [P, HALF], U32)
-            nc.vector.tensor_copy(gw[:], xw[:].indirect(entries(offs_t, h)))
+        for half in range(2):
+            picked_words = sbuf("picked_words%d" % half, [P, HALF], U32)
+            nc.vector.tensor_copy(picked_words[:], table_words[:].indirect(entries(offs_t, half)))
             for pair in range(2):
-                acc = bank()
+                bank = pair_bank()
                 for i in range(2):
-                    y[h, 2 * pair + i] = acc[:, i * HALF : (i + 1) * HALF]
-                    product(y[h, 2 * pair + i], w1_q[pair], i, gw[:], gs[:, h * HALF : (h + 1) * HALF])
+                    y[half, 2 * pair + i] = bank[:, i * HALF : (i + 1) * HALF]
+                    product(y[half, 2 * pair + i], w1_q[pair], i, picked_words[:], picked_scales[:, half_cols(half)])
             for t in range(PACK):
-                nc.scalar.activation(pw[t][:, h * HALF : (h + 1) * HALF], y[h, t], ACT.Square)
+                nc.scalar.activation(pw[t][:, half_cols(half)], y[half, t], ACT.Square)
 
-        old = [sb("old%d" % t, [P, S], F32) for t in range(PACK)]
+        old = [sbuf("old%d" % t, [P, S], F32) for t in range(PACK)]
         for t in range(PACK):
             nc.vector.tensor_copy(old[t][:], page[t][:].indirect(slot_t[:]))
 
-        def gate(h):
-            e = [sb("e%d_%d" % (h, t), [P, HALF], F32) for t in range(PACK)]
+        def gates(half):
+            gate = [sbuf("gate%d_%d" % (half, t), [P, HALF], F32) for t in range(PACK)]
             for t in range(PACK):
-                nc.scalar.activation(e[t][:], pw[t][:].indirect(entries(n1_t, h)), ACT.Exp, scale=-0.5)
-            return e
+                nc.scalar.activation(gate[t][:], pw[t][:].indirect(entries(n1_t, half)), ACT.Exp, scale=-0.5)
+            return gate
 
-        def z_planes(h, e, planes, tiles):
+        def form_z(half, gate, z_tiles, tiles):
             for t in tiles:
-                nc.vector.scalar_tensor_tensor(planes[:, t * HALF : (t + 1) * HALF], y[h, t], gn_t[:, t : t + 1], e[t][:], ALU.mult, ALU.mult)
+                nc.vector.scalar_tensor_tensor(
+                    z_tiles[:, t * HALF : (t + 1) * HALF], y[half, t], gn_t[:, t : t + 1], gate[t][:], ALU.mult, ALU.mult
+                )
 
-        def z_weave(h, planes, engine):
-            grouped = sb("z_bf%d" % h, [P, PACK * HALF], BF16, "after_first" if h == 1 else "")
+        def weave_views(half, z_tiles, tag=""):
+            grouped = sbuf("z_bf%d" % half, [P, PACK * HALF], BF16, tag)
             dst = grouped[:].rearrange("p (c i t) -> p c t i", i=4, t=PACK)
-            src = planes[:].rearrange("p (t c i) -> p c t i", i=4, t=PACK)
-            if engine == "scalar":
-                nc.scalar.copy(dst, src)
-            else:
-                nc.vector.tensor_copy(dst, src)
-            return grouped
+            src = z_tiles[:].rearrange("p (t c i) -> p c t i", i=4, t=PACK)
+            return grouped, dst, src
 
-        hh = {}
+        h = {}
 
-        def second(h, pair, zq):
-            acc = bank()
+        def second_layer(half, pair, z_q):
+            bank = pair_bank()
             for i in range(2):
-                hh[h, 2 * pair + i] = acc[:, i * HALF : (i + 1) * HALF]
-                if (h, pair, i) == (0, 0, 0):
-                    hh[0, 0] = psum.tile([P, HALF], F32, name="back")[:]
-                product(hh[h, 2 * pair + i], w2_q[pair], i, zq[0][:], zq[1][:])
+                t = 2 * pair + i
+                h[half, t] = bank[:, i * HALF : (i + 1) * HALF]
+                if (half, t) == (0, 0):
+                    h[half, t] = psum.tile([P, HALF], F32, name="back")[:]
+                product(h[half, t], w2_q[pair], i, z_q[0][:], z_q[1][:])
 
-        def step_vector(h, t):
-            return finish(h, t, subtract(h, t))
+        def move_on_vector(half, t):
+            diff = sbuf("diff%d_%d" % (half, t), [P, HALF], F32)
+            nc.vector.tensor_tensor(diff[:], h[half, t], old[t][:, half_cols(half)], ALU.subtract)
+            tanh = sbuf("tanh%d_%d" % (half, t), [P, HALF], F32, "first_tanh" if (half, t) == (0, 0) else "")
+            nc.scalar.activation(tanh[:], diff[:], ACT.Tanh)
+            move = sbuf("move%d_%d" % (half, t), [P, HALF], F32)
+            nc.scalar.activation(move[:], tanh[:], ACT.Copy, scale=0.5)
+            return move
 
-        def subtract(h, t):
-            diff = sb("diff%d_%d" % (h, t), [P, HALF], F32)
-            nc.vector.tensor_tensor(diff[:], hh[h, t], old[t][:, h * HALF : (h + 1) * HALF], ALU.subtract)
-            return diff
-
-        def finish(h, t, diff):
-            th = sb("th%d_%d" % (h, t), [P, HALF], F32, "after_first" if (h, t) == (0, 0) else "")
-            nc.scalar.activation(th[:], diff[:], ACT.Tanh)
-            step = sb("step%d_%d" % (h, t), [P, HALF], F32)
-            nc.scalar.activation(step[:], th[:], ACT.Copy, scale=0.5)
-            return step
-
-        def step_tensor(h, t):
-            neg = sb("neg%d_%d" % (h, t), [P, HALF], F32)
-            nc.scalar.activation(neg[:], hh[h, t], ACT.Copy, scale=-1.0)
+        def move_on_tensor(half, t):
+            minus_h = sbuf("minus_h%d_%d" % (half, t), [P, HALF], F32)
+            nc.scalar.activation(minus_h[:], h[half, t], ACT.Copy, scale=-1.0)
             turned = psum.tile([P, HALF], F32, name="turned")
-            for b in range(2):
+            for b in range(HALF // P):
                 cols = slice(b * P, (b + 1) * P)
-                first = h * HALF + b * P
-                nc.tensor.matmul(turned[:, cols], old[t][:, first : first + P], ident[:], start=True, stop=False, is_transpose=True)
-                nc.tensor.matmul(turned[:, cols], neg[:, cols], ident[:], start=False, stop=True, is_transpose=True)
-            th = sb("th%d_%d" % (h, t), [P, HALF], F32)
-            nc.scalar.activation(th[:], turned[:], ACT.Tanh, scale=-1.0)
+                first = half * HALF + b * P
+                nc.tensor.matmul(turned[:, cols], old[t][:, first : first + P], identity[:], start=True, stop=False, is_transpose=True)
+                nc.tensor.matmul(turned[:, cols], minus_h[:, cols], identity[:], start=False, stop=True, is_transpose=True)
+            tanh = sbuf("tanh%d_%d" % (half, t), [P, HALF], F32)
+            nc.scalar.activation(tanh[:], turned[:], ACT.Tanh, scale=-1.0)
             back = psum.tile([P, HALF], F32, name="back")
-            for b in range(2):
+            for b in range(HALF // P):
                 cols = slice(b * P, (b + 1) * P)
-                nc.tensor.transpose(back[:, cols], th[:, cols], ident[:])
-            step = sb("step%d_%d" % (h, t), [P, HALF], F32)
-            nc.scalar.activation(step[:], back[:], ACT.Copy, scale=0.5)
-            return step
+                nc.tensor.transpose(back[:, cols], tanh[:, cols], identity[:])
+            move = sbuf("move%d_%d" % (half, t), [P, HALF], F32)
+            nc.scalar.activation(move[:], back[:], ACT.Copy, scale=0.5)
+            return move
 
-        def put(h, t, step):
-            nc.vector.tensor_tensor(page[t][:].indirect(entries(slot_t, h)), old[t][:, h * HALF : (h + 1) * HALF], step[:], ALU.add)
-            if h == 1:
-                nc.sync.dma_start(out_rows[:, t, :], page[t][:])
+        def move_of(half, t):
+            return move_on_vector(half, t) if (half, t) in SUBTRACT_ON_VECTOR else move_on_tensor(half, t)
 
-        ON_VECTOR = (0,1,2,4,)
+        def put(half, t):
+            nc.vector.tensor_tensor(page[t][:].indirect(entries(slot_t, half)), old[t][:, half_cols(half)], moves[half, t][:], ALU.add)
 
-        def step_of(h, t):
-            return step_vector(h, t) if 4 * h + t in ON_VECTOR else step_tensor(h, t)
+        gate0 = gates(0)
+        gate1 = gates(1)
 
-        e0 = gate(0)
-        e1 = gate(1)
-        planes0 = sb("zp0", [P, PACK * HALF], BF16)
-        z_planes(0, e0, planes0, range(PACK))
-        woven0 = z_weave(0, planes0, "vector")
-        w2_bf = [deal(w2_raw, 0, "w2", "vector", "held"), deal(w2_raw, 1, "w2", "scalar")]
-        z0 = quantize(woven0, "z0")
+        z_tiles0 = sbuf("z_tiles0", [P, PACK * HALF], BF16)
+        form_z(0, gate0, z_tiles0, range(PACK))
+        w2_bf = deal(w2_raw, "w2", "w2_first")
+        z_bf0, dst, src = weave_views(0, z_tiles0)
+        nc.vector.tensor_copy(dst, src)
         w2_q = {0: quantize(w2_bf[0], "w2_0")}
-        second(0, 0, z0)
-        steps = {}
-        steps[0, 0] = step_of(0, 0)
-        planes1 = sb("zp1", [P, PACK * HALF], BF16, "held")
-        z_planes(1, e1, planes1, (0, 1))
+        z_q0 = quantize(z_bf0, "z0")
+        second_layer(0, 0, z_q0)
+        moves = {(0, 0): move_of(0, 0)}
+
+        z_tiles1 = sbuf("z_tiles1", [P, PACK * HALF], BF16, "w2_first")
+        form_z(1, gate1, z_tiles1, (0, 1))
         w2_q[1] = quantize(w2_bf[1], "w2_1")
-        second(0, 1, z0)
-        z_planes(1, e1, planes1, (2, 3))
-        woven1 = z_weave(1, planes1, "scalar")
+        second_layer(0, 1, z_q0)
+        form_z(1, gate1, z_tiles1, (2, 3))
+        z_bf1, dst, src = weave_views(1, z_tiles1, "first_tanh")
+        nc.scalar.copy(dst, src)
         for t in (1, 3, 2):
-            steps[0, t] = step_of(0, t)
-        z1 = quantize(woven1, "z1")
-        second(1, 0, z1)
-        second(1, 1, z1)
+            moves[0, t] = move_of(0, t)
+        z_q1 = quantize(z_bf1, "z1")
+        second_layer(1, 0, z_q1)
+        second_layer(1, 1, z_q1)
+
         for t in range(PACK):
-            put(0, t, steps[0, t])
-            steps[1, t] = step_of(1, t)
+            put(0, t)
+            moves[1, t] = move_of(1, t)
         for t in range(PACK):
-            put(1, t, steps[1, t])
+            put(1, t)
+            nc.sync.dma_start(out_rows[:, t, :], page[t][:])

from contextlib import ExitStack

import concourse.mybir as mybir
from concourse.masks import make_identity

K, T, S, N, H, U = 512, 2048, 512, 512, 512, 1024
FLOPS = 2 * K * H * S + 2 * H * N * S

F32 = mybir.dt.float32
BF16 = mybir.dt.bfloat16
I32 = mybir.dt.int32
U32 = mybir.dt.uint32
U16 = mybir.dt.uint16
U8 = mybir.dt.uint8
FP8X4 = mybir.dt.float8_e4m3fn_x4
ALU = mybir.AluOpType
ACT = mybir.ActivationFunctionType

P = 128
PACK = 4
HALF = S // 2
LIST_COLS = HALF // 16
PAIR_BANKS = 4
TURN_BANKS = 2

SUBTRACT_ON_VECTOR = ((0, 0), (0, 1), (0, 2), (1, 0))


def tile_picked_masktrack_none_p_kernel(tc, x_words, x_scales, w1, gn, w2, pg, offs, n1, slot, out):
    nc = tc.nc
    with ExitStack() as ctx:
        keep = ctx.enter_context(tc.tile_pool(name="keep", bufs=1))
        psum = ctx.enter_context(tc.psum_pool(name="psum", bufs=TURN_BANKS))

        def sbuf(name, shape, dtype, tag=""):
            return keep.tile(shape, dtype, name=name, tag=tag, align_bytes=64)

        def pair_bank():
            return psum.tile([P, 2 * HALF], F32, name="pair_bank", bufs=PAIR_BANKS)

        def half_cols(half):
            return slice(half * HALF, (half + 1) * HALF)

        def entries(list_tile, half):
            return list_tile[:, half * LIST_COLS : (half + 1) * LIST_COLS]

        offs_t = sbuf("offs_t", [P, S // 16], U16)
        n1_t = sbuf("n1_t", [P, S // 16], U16)
        slot_t = sbuf("slot_t", [P, S // 16], U16)
        table_words = sbuf("table_words", [P, T], U32)
        table_scales = sbuf("table_scales", [P, T], U8)
        w1_raw = sbuf("w1_raw", [P, PACK, H], F32)
        w2_raw = sbuf("w2_raw", [P, PACK, N], F32)
        gn_t = sbuf("gn_t", [P, PACK], F32)
        page = [sbuf("page%d" % t, [P, U], F32) for t in range(PACK)]
        identity = sbuf("identity", [P, P], F32)

        nc.vector.memset(table_scales[:].bitcast(I32), 0)
        make_identity(nc, identity[:])

        pg_rows = pg.rearrange("(p t) u -> p t u", t=PACK)
        out_rows = out.rearrange("(p t) u -> p t u", t=PACK)
        w2_rows = w2.rearrange("(p j) c -> p j c", j=PACK)
        nc.sync.dma_start(offs_t[:], offs)
        nc.sync.dma_start(w1_raw[:], w1.rearrange("(p j) c -> p j c", j=PACK))
        for q in range(4):
            nc.sync.dma_start(table_scales[32 * q : 32 * q + 4, :].bitcast(I32), x_scales[0, 4 * q : 4 * q + 4, :].bitcast(I32))
        nc.sync.dma_start(table_words[:].bitcast(I32), x_words[0].rearrange("p n r -> p (n r)").bitcast(I32))
        nc.sync.dma_start(slot_t[:], slot)
        nc.sync.dma_start(n1_t[:], n1)
        for t in range(PACK):
            nc.sync.dma_start(page[t][:], pg_rows[:, t, :])
        nc.sync.dma_start(w2_raw[:, 0:2, :], w2_rows[:, 0:2, :])
        nc.sync.dma_start(gn_t[:], gn.rearrange("(p t) o -> p (t o)", t=PACK))
        nc.sync.dma_start(w2_raw[:, 2:4, :], w2_rows[:, 2:4, :])

        def deal_views(raw, pair, name, tag=""):
            grouped = sbuf("%s_bf%d" % (name, pair), [P, 2 * P * PACK], BF16, tag)
            dst = grouped[:].rearrange("p (t m j) -> p m j t", t=2, j=PACK)
            src = raw[:].rearrange("p j (m t) -> p m j t", t=PACK)[:, :, :, 2 * pair : 2 * pair + 2]
            return grouped, dst, src

        def deal(raw, name, first_tag=""):
            first, dst, src = deal_views(raw, 0, name, first_tag)
            nc.vector.tensor_copy(dst, src)
            second, dst, src = deal_views(raw, 1, name)
            nc.scalar.activation(dst, src, ACT.Copy)
            return first, second

        def quantize(grouped, name):
            width = grouped.shape[1] // PACK
            words = sbuf(name + "_words", [P, width], U32)
            scales = sbuf(name + "_scales", [P, width], U8)
            nc.vector.quantize_mx(out=words[:].bitcast(FP8X4), scales=scales[:], in_=grouped[:])
            return words, scales

        def product(dst, weights, i, words, scales):
            cols = slice(i * P, (i + 1) * P)
            nc.tensor.matmul_mx(
                out=dst,
                lhsT=weights[0][:, cols].bitcast(FP8X4),
                lhsT_scale=weights[1][:, cols],
                rhs=words.bitcast(FP8X4),
                rhs_scale=scales,
                start=True,
                stop=True,
            )

        picked_scales = sbuf("picked_scales", [P, S], U8)
        nc.vector.tensor_copy(picked_scales[:], table_scales[:].indirect(offs_t[:]))
        w1_bf = deal(w1_raw, "w1")
        w1_q = [quantize(w1_bf[pair], "w1_%d" % pair) for pair in range(2)]
        pw = [sbuf("pw%d" % t, [P, S], F32) for t in range(PACK)]
        y = {}
        for half in range(2):
            picked_words = sbuf("picked_words%d" % half, [P, HALF], U32)
            nc.vector.tensor_copy(picked_words[:], table_words[:].indirect(entries(offs_t, half)))
            for pair in range(2):
                bank = pair_bank()
                for i in range(2):
                    y[half, 2 * pair + i] = bank[:, i * HALF : (i + 1) * HALF]
                    product(y[half, 2 * pair + i], w1_q[pair], i, picked_words[:], picked_scales[:, half_cols(half)])
            for t in range(PACK):
                nc.scalar.activation(pw[t][:, half_cols(half)], y[half, t], ACT.Square)

        old = [sbuf("old%d" % t, [P, S], F32) for t in range(PACK)]
        for t in range(PACK):
            nc.vector.tensor_copy(old[t][:], page[t][:].indirect(slot_t[:]))

        def gates(half):
            gate = [sbuf("gate%d_%d" % (half, t), [P, HALF], F32) for t in range(PACK)]
            for t in range(PACK):
                nc.scalar.activation(gate[t][:], pw[t][:].indirect(entries(n1_t, half)), ACT.Exp, scale=-0.5)
            return gate

        def form_z(half, gate, z_tiles, tiles):
            for t in tiles:
                nc.vector.scalar_tensor_tensor(
                    z_tiles[:, t * HALF : (t + 1) * HALF], y[half, t], gn_t[:, t : t + 1], gate[t][:], ALU.mult, ALU.mult
                )

        def weave_views(half, z_tiles, tag=""):
            grouped = sbuf("z_bf%d" % half, [P, PACK * HALF], BF16, tag)
            dst = grouped[:].rearrange("p (c i t) -> p c t i", i=4, t=PACK)
            src = z_tiles[:].rearrange("p (t c i) -> p c t i", i=4, t=PACK)
            return grouped, dst, src

        h = {}

        def second_layer(half, pair, z_q):
            bank = pair_bank()
            for i in range(2):
                t = 2 * pair + i
                h[half, t] = bank[:, i * HALF : (i + 1) * HALF]
                if (half, t) == (0, 0):
                    h[half, t] = psum.tile([P, HALF], F32, name="back")[:]
                product(h[half, t], w2_q[pair], i, z_q[0][:], z_q[1][:])

        def move_on_vector(half, t):
            diff = sbuf("diff%d_%d" % (half, t), [P, HALF], F32)
            nc.vector.tensor_tensor(diff[:], h[half, t], old[t][:, half_cols(half)], ALU.subtract)
            tanh = sbuf("tanh%d_%d" % (half, t), [P, HALF], F32, "first_tanh" if (half, t) == (0, 0) else "")
            nc.scalar.activation(tanh[:], diff[:], ACT.Tanh)
            move = sbuf("move%d_%d" % (half, t), [P, HALF], F32)
            nc.scalar.activation(move[:], tanh[:], ACT.Copy, scale=0.5)
            return move

        def move_on_tensor(half, t):
            minus_h = sbuf("minus_h%d_%d" % (half, t), [P, HALF], F32)
            nc.scalar.activation(minus_h[:], h[half, t], ACT.Copy, scale=-1.0)
            turned = psum.tile([P, HALF], F32, name="turned")
            for b in range(HALF // P):
                cols = slice(b * P, (b + 1) * P)
                first = half * HALF + b * P
                nc.tensor.matmul(turned[:, cols], old[t][:, first : first + P], identity[:], start=True, stop=False, is_transpose=True)
                nc.tensor.matmul(turned[:, cols], minus_h[:, cols], identity[:], start=False, stop=True, is_transpose=True)
            tanh = sbuf("tanh%d_%d" % (half, t), [P, HALF], F32)
            nc.scalar.activation(tanh[:], turned[:], ACT.Tanh, scale=-1.0)
            back = psum.tile([P, HALF], F32, name="back")
            for b in range(HALF // P):
                cols = slice(b * P, (b + 1) * P)
                nc.tensor.transpose(back[:, cols], tanh[:, cols], identity[:])
            move = sbuf("move%d_%d" % (half, t), [P, HALF], F32)
            nc.scalar.activation(move[:], back[:], ACT.Copy, scale=0.5)
            return move

        def move_of(half, t):
            return move_on_vector(half, t) if (half, t) in SUBTRACT_ON_VECTOR else move_on_tensor(half, t)

        def put(half, t):
            nc.vector.tensor_tensor(page[t][:].indirect(entries(slot_t, half)), old[t][:, half_cols(half)], moves[half, t][:], ALU.add)

        gate0 = gates(0)
        gate1 = gates(1)

        z_tiles0 = sbuf("z_tiles0", [P, PACK * HALF], BF16)
        form_z(0, gate0, z_tiles0, range(PACK))
        w2_bf = deal(w2_raw, "w2", "w2_first")
        z_bf0, dst, src = weave_views(0, z_tiles0)
        nc.vector.tensor_copy(dst, src)
        w2_q = {0: quantize(w2_bf[0], "w2_0")}
        z_q0 = quantize(z_bf0, "z0")
        second_layer(0, 0, z_q0)
        moves = {(0, 0): move_of(0, 0)}

        z_tiles1 = sbuf("z_tiles1", [P, PACK * HALF], BF16, "w2_first")
        form_z(1, gate1, z_tiles1, (0, 1))
        w2_q[1] = quantize(w2_bf[1], "w2_1")
        second_layer(0, 1, z_q0)
        form_z(1, gate1, z_tiles1, (2, 3))
        z_bf1, dst, src = weave_views(1, z_tiles1, "first_tanh")
        nc.scalar.copy(dst, src)
        for t in (1, 3, 2):
            moves[0, t] = move_of(0, t)
        z_q1 = quantize(z_bf1, "z1")
        second_layer(1, 0, z_q1)
        second_layer(1, 1, z_q1)

        for t in range(PACK):
            put(0, t)
            moves[1, t] = move_of(1, t)
        for t in range(PACK):
            put(1, t)
            nc.sync.dma_start(out_rows[:, t, :], page[t][:])
